import numpy as np
import ml_dtypes


def mxq(x, axis, fmt="e4m3"):
    dtype, down = {"e4m3": (ml_dtypes.float8_e4m3fn, 7), "e5m2": (ml_dtypes.float8_e5m2, 14)}[fmt]
    v = np.moveaxis(np.asarray(x, np.float32).astype(ml_dtypes.bfloat16).astype(np.float64), axis, -1)
    blocks = v.reshape(v.shape[:-1] + (-1, 32))
    amax = np.abs(blocks).max(-1, keepdims=True)
    byte = np.maximum(np.where(amax > 0, np.frexp(amax)[1] - 1 + 127, 0) - down, 1)
    scale = np.exp2(byte - 127.0)
    codes = (blocks / scale).astype(np.float32).astype(dtype).astype(np.float64)
    return np.moveaxis((codes * scale).reshape(v.shape), -1, axis)


WIDE = False


def mx_kscale(k):
    if not WIDE:
        return np.ones(k)
    levels = np.array([10, -10, 5, -5, 0])
    if k % 512:
        return np.exp2(np.random.permutation(np.resize(levels, k // 32))).repeat(32)
    a = np.empty((k // 512, 16))
    for p in range(k // 512):
        a[p, :8] = np.random.permutation(np.resize(levels, 8))
        for g in range(8):
            far = levels[np.abs(levels - a[p, g]) >= 10]
            a[p, g + 8] = far[np.random.randint(len(far))]
    return np.exp2(a.ravel()).repeat(32)


BF16 = ml_dtypes.bfloat16


def bf(x):
    return np.asarray(x, np.float32).astype(BF16)


def f64(x):
    return np.asarray(x).astype(np.float64)

E4M3FN = np.array([(-1.0 if i & 128 else 1.0) * ((1.0 + (i & 7) / 8.0) * 2.0 ** (((i >> 3) & 15) - 7) if i & 120 else (i & 7) * 2.0 ** -9) for i in range(256)])


def e4m3fn_bytes(y):
    return np.clip(np.asarray(y, np.float64), -448.0, 448.0).astype(np.float32).astype(ml_dtypes.float8_e4m3fn).view(np.uint8)


def e4m3fn_values(b):
    return E4M3FN[b]


T, D, DK, DV, B = 1024, 2048, 1024, 1024, 128
FP8_MAX = 448.0


def setup_inputs():
    s, t = mx_kscale(D), mx_kscale(DK)
    w = np.random.standard_normal((D, DK)) / np.sqrt(D) / s[:, None]
    w_scale = (np.abs(w).reshape(D // B, B, DK // B, B).max(axis=(1, 3)) / FP8_MAX).astype(np.float32)
    w_bytes = e4m3fn_bytes(w / np.repeat(np.repeat(f64(w_scale), B, axis=0), B, axis=1))
    state = np.random.standard_normal((DV, DK)) * np.sqrt(2.0 / DK) / t
    state_scale = (np.abs(state).reshape(DV // B, B, DK // B, B).max(axis=(1, 3)) / FP8_MAX).astype(np.float32)
    state_bytes = e4m3fn_bytes(state / np.repeat(np.repeat(f64(state_scale), B, axis=0), B, axis=1))
    return {"x": bf(np.random.standard_normal((T, D)) * s),
            "w_bytes": w_bytes,
            "w_scale": w_scale,
            "gain": bf((1.0 + 0.1 * np.random.standard_normal(DK)) * t),
            "state_bytes": state_bytes,
            "state_scale": state_scale,
            "v": bf(np.random.standard_normal((T, DV))),
            "beta": bf(np.random.uniform(0.2, 1.0, (T, 1)))}


def reference(x, w_bytes, w_scale, gain, state_bytes, state_scale, v, beta):
    w = e4m3fn_values(w_bytes) * np.repeat(np.repeat(f64(w_scale), B, axis=0), B, axis=1)
    state = e4m3fn_values(state_bytes) * np.repeat(np.repeat(f64(state_scale), B, axis=0), B, axis=1)
    h = mxq(f64(x), 1, "e4m3") @ mxq(w, 0, "e4m3")
    key = np.maximum(h, 0.0) * f64(gain)
    read = mxq(key, 1, "e4m3") @ mxq(state, 1, "e4m3").T
    return f64(beta) * (f64(v) - read)

@@ -1,0 +1,352 @@
+from contextlib import ExitStack
+
+import concourse.mybir as mybir
+from concourse.masks import make_identity
+
+T, D, DK, DV = 1024, 2048, 1024, 1024
+FLOPS = 2 * T * D * DK + 2 * T * DK * DV
+
+F32 = mybir.dt.float32
+BF16 = mybir.dt.bfloat16
+U32 = mybir.dt.uint32
+U8 = mybir.dt.uint8
+FP8 = mybir.dt.float8_e4m3fn
+FP8X4 = mybir.dt.float8_e4m3fn_x4
+ALU = mybir.AluOpType
+COPY = mybir.ActivationFunctionType.Copy
+
+P = 128
+PACK = 4
+KP = P * PACK
+SB = 128
+TILES = T // P
+XG = D // KP
+KH = DK // KP
+DH = DV // KP
+BANKS = 8
+
+
+def tile_delta_memory_error_d7_kernel(tc, x, w_bytes, w_scale, gain, state_bytes, state_scale, v, beta, out):
+    nc = tc.nc
+    x_t = x.rearrange("(p i) k -> i p k", i=TILES)
+    v_t = v.rearrange("(p i) c -> i p c", i=TILES)
+    out_t = out.rearrange("(p i) c -> i p c", i=TILES)
+
+    with ExitStack() as ctx:
+        keep = ctx.enter_context(tc.tile_pool(name="keep", bufs=1))
+        ring = ctx.enter_context(tc.tile_pool(name="ring", bufs=3))
+        psum = ctx.enter_context(tc.psum_pool(name="psum", bufs=1))
+        ctx.enter_context(tc.manual_schedule())
+
+        banks_taken = []
+
+        def next_bank():
+            n = len(banks_taken)
+            bank = psum.tile([P, KP], F32, name="bank", tag="bank%d" % (n % BANKS))
+            banks_taken.append(n)
+            return bank
+
+        def kept(shape, dtype, name):
+            return keep.tile(shape, dtype, name=name, tag=name, align_bytes=64)
+
+        def ringed(shape, dtype, name, bufs):
+            return ring.tile(shape, dtype, name=name, tag=name, bufs=bufs, align_bytes=64)
+
+        w_raw, x_raw, s_raw, v_raw = {}, {}, {}, {}
+
+        def load_w(h, g):
+            w_raw[h, g] = kept([P, PACK * KP], U8, "wbytes%d%d" % (h, g))
+            nc.sync.dma_start(
+                out=w_raw[h, g][:].rearrange("p (j c) -> p j c", j=PACK),
+                in_=w_bytes[g * KP : (g + 1) * KP, h * KP : (h + 1) * KP].rearrange("(p j) c -> p j c", j=PACK),
+            )
+
+        def load_x(i):
+            x_raw[i] = kept([P, D // 2], F32, "xwords%d" % i)
+            nc.sync.dma_start(out=x_raw[i][:], in_=x_t[i].bitcast(F32))
+
+        def load_state(d):
+            s_raw[d] = kept([P, PACK * DK], U8, "sbytes%d" % d)
+            nc.sync.dma_start(
+                out=s_raw[d][:].rearrange("p (r k) -> p r k", r=PACK),
+                in_=state_bytes[d * KP : (d + 1) * KP, :].rearrange("(r p) k -> p r k", p=P),
+            )
+
+        def load_v(i):
+            v_raw[i] = kept([P, DV], BF16, "v%d" % i)
+            nc.sync.dma_start(out=v_raw[i][:], in_=v_t[i])
+
+        ident = kept([P, P], F32, "ident")
+        make_identity(nc, ident[:])
+
+        beta_sb = kept([P, TILES], BF16, "beta")
+        nc.scalar.dma_start(out=beta_sb[:], in_=beta.rearrange("(p i) o -> p (i o)", i=TILES))
+        ws_col = kept([P, 1], F32, "wscol")
+        nc.scalar.dma_start(out=ws_col[:], in_=w_scale.rearrange("a (b o) -> (a b) o", o=1))
+        ss_col = kept([P, 1], F32, "sscol")
+        nc.vector.memset(ss_col[:], 0.0)
+        gain_col = kept([P, KH * PACK], BF16, "gaincol")
+
+        load_w(0, 0)
+        load_w(0, 1)
+        load_x(0)
+        load_w(0, 2)
+        load_w(0, 3)
+        load_x(1)
+        nc.sync.dma_start(out=gain_col[:].rearrange("p (h t) -> p h t", t=PACK), in_=gain.rearrange("(h p t) -> p h t", p=P, t=PACK))
+        load_x(2)
+        for g in range(XG):
+            load_w(1, g)
+            load_x(3 + g)
+            if g == 1:
+                nc.sync.dma_start(out=ss_col[0:64, :], in_=state_scale.rearrange("a (b o) -> (a b) o", o=1))
+        load_state(0)
+        load_x(7)
+        load_state(1)
+        for i in range(TILES):
+            load_v(i)
+
+        nbeta = kept([P, TILES], F32, "nbeta")
+        nc.scalar.activation(out=nbeta[:], in_=beta_sb[:], func=COPY, scale=-1.0)
+
+        ws = kept([P, XG * 8], F32, "ws")
+        bank = next_bank()
+        nc.tensor.transpose(bank[:, 0:P], ws_col[:, 0:1].to_broadcast([P, P]), ident[:])
+        ws_spread = bank[:, 0:P].rearrange("p (g q b) -> p q g b", g=XG, q=4)
+
+        def pick_w_scales():
+            for q in range(4):
+                nc.vector.tensor_copy(out=ws[32 * q : 32 * q + 32, :].rearrange("p (g b) -> p g b", g=XG), in_=ws_spread[32 * q : 32 * q + 32, q])
+
+        w_wide, w_grp, w_codes, w_scales = {}, {}, {}, {}
+
+        def widen_w(h, g, on_vector=False):
+            w_wide[h, g] = ringed([P, PACK * KP], BF16, "wwide", 3)
+            if on_vector:
+                nc.vector.tensor_copy(out=w_wide[h, g][:], in_=w_raw[h, g][:].bitcast(FP8))
+            else:
+                nc.scalar.copy(out=w_wide[h, g][:], in_=w_raw[h, g][:].bitcast(FP8))
+
+        def group_w(h, g):
+            w_grp[h, g] = ringed([P, PACK * KP], BF16, "wgrp", 2)
+            src = w_wide[h, g][:].rearrange("p (j m t) -> p m j t", j=PACK, t=PACK)
+            dst = w_grp[h, g][:].rearrange("p (t m j) -> p m j t", j=PACK, t=PACK)
+            for b in range(KP // SB):
+                col = g * 8 + h * 4 + b
+                nc.vector.tensor_scalar(
+                    out=dst[:, 32 * b : 32 * b + 32], in0=src[:, 32 * b : 32 * b + 32],
+                    scalar1=ws[:, col : col + 1], scalar2=None, op0=ALU.mult,
+                )
+
+        def quantize(src, name):
+            width = src.shape[1] // PACK
+            codes = kept([P, width], U32, name + "c")
+            scales = kept([P, width], U8, name + "s")
+            nc.vector.quantize_mx(out=codes[:].bitcast(FP8X4), scales=scales[:], in_=src)
+            return codes, scales
+
+        def quant_w(h, g):
+            w_codes[h, g], w_scales[h, g] = quantize(w_grp[h, g][:], "wq%d%d" % (h, g))
+
+        def turn(words):
+            bank = next_bank()
+            for n in range(4):
+                g, u = divmod(n, 2)
+                nc.tensor.transpose(bank[:, n * P : (n + 1) * P], words[:, 256 * g + u : 256 * (g + 1) : 2], ident[:])
+            return bank
+
+        x_bank, x_grp, x_q = {}, {}, {}
+
+        def turn_x(i):
+            for a in range(2):
+                x_bank[i, a] = turn(x_raw[i][:, a * KP : (a + 1) * KP])
+
+        def empty_x(i):
+            x_grp[i] = ringed([P, D // 2], F32, "xgrp", 3)
+            for a in range(2):
+                nc.scalar.copy(
+                    out=x_grp[i][:, a * KP : (a + 1) * KP].rearrange("p (g r u) -> p g r u", g=2, u=2),
+                    in_=x_bank[i, a][:].rearrange("p (g u r) -> p g r u", g=2, u=2),
+                )
+
+        def quant_x(i):
+            x_q[i] = quantize(x_grp[i][:].bitcast(BF16), "xq%d" % i)
+
+        gain_wide = kept([P, KH * KP], BF16, "gainwide")
+
+        def spread_gain():
+            for h in range(KH):
+                nc.vector.tensor_copy(
+                    out=gain_wide[:, h * KP : (h + 1) * KP].rearrange("p (n t) -> p n t", t=PACK),
+                    in_=gain_col[:, h * PACK : (h + 1) * PACK].unsqueeze(1).to_broadcast([P, P, PACK]),
+                )
+
+        h_bank, key, key_q = {}, {}, {}
+
+        def project(i, h):
+            h_bank[i, h] = next_bank()
+            xc, xs = x_q[i]
+            for t in range(PACK):
+                cols = slice(t * P, (t + 1) * P)
+                for g in range(XG):
+                    toks = slice(g * P, (g + 1) * P)
+                    nc.tensor.matmul_mx(
+                        out=h_bank[i, h][:, cols],
+                        lhsT=w_codes[h, g][:, cols].bitcast(FP8X4), lhsT_scale=w_scales[h, g][:, cols],
+                        rhs=xc[:, toks].bitcast(FP8X4), rhs_scale=xs[:, toks],
+                        start=(g == 0), stop=(g == XG - 1),
+                    )
+
+        def make_key(i, h):
+            key[i, h] = ringed([P, KP], BF16, "key", 4)
+            nc.vector.scalar_tensor_tensor(
+                out=key[i, h][:].rearrange("p (n t) -> p n t", t=PACK),
+                in0=h_bank[i, h][:].rearrange("p (t n) -> p n t", t=PACK),
+                scalar=0.0,
+                in1=gain_wide[:, h * KP : (h + 1) * KP].rearrange("p (n t) -> p n t", t=PACK),
+                op0=ALU.max, op1=ALU.mult,
+            )
+
+        def quant_key(i, h):
+            key_q[i, h] = quantize(key[i, h][:], "kq%d%d" % (i, h))
+
+        ss = kept([P, 64], F32, "ss")
+        s_wide, s_bank, s_grp, s_q = {}, {}, {}, {}
+
+        def spread_state_scales():
+            bank = next_bank()
+            nc.tensor.transpose(bank[:, 0:P], ss_col[:, 0:1].to_broadcast([P, P]), ident[:])
+            nc.scalar.copy(out=ss[:], in_=bank[:, 0:64])
+
+        def widen_state(r, on_vector=False):
+            d, rr = divmod(r, PACK)
+            s_wide[r] = ringed([P, DK], BF16, "swide", 4)
+            for b in range(DK // SB):
+                src = s_raw[d][:, rr * DK + b * SB : rr * DK + (b + 1) * SB].bitcast(FP8)
+                dst = s_wide[r][:, b * SB : (b + 1) * SB]
+                col = r * 8 + b
+                if on_vector:
+                    nc.vector.tensor_scalar(out=dst, in0=src, scalar1=ss[:, col : col + 1], scalar2=None, op0=ALU.mult)
+                else:
+                    nc.scalar.activation(out=dst, in_=src, func=COPY, scale=ss[:, col : col + 1])
+
+        def turn_state(r):
+            s_bank[r] = turn(s_wide[r][:].bitcast(F32))
+
+        def empty_state(r):
+            d, rr = divmod(r, PACK)
+            if rr == 0:
+                s_grp[d] = kept([P, KH * KP * 2], F32, "sgrp%d" % d)
+            nc.scalar.copy(
+                out=s_grp[d][:].rearrange("p (h a r u) -> p a h r u", h=KH, a=PACK, u=2)[:, rr],
+                in_=s_bank[r][:].rearrange("p (h u r) -> p h r u", h=KH, u=2),
+            )
+
+        def quant_state(d, h):
+            s_q[d, h] = quantize(s_grp[d][:, h * 2 * KP : (h + 1) * 2 * KP].bitcast(BF16), "sq%d%d" % (d, h))
+
+        nbv, r_bank, res = {}, {}, {}
+
+        def scale_v(i, d):
+            nbv[i, d] = ringed([P, KP], F32, "nbv", 6)
+            nc.scalar.activation(out=nbv[i, d][:], in_=v_raw[i][:, d * KP : (d + 1) * KP], func=COPY, scale=nbeta[:, i : i + 1])
+
+        def read_memory(i, d):
+            r_bank[i, d] = next_bank()
+            for h in range(KH):
+                kc, ks = key_q[i, h]
+                sc, sk = s_q[d, h]
+                nc.tensor.matmul_mx(
+                    out=r_bank[i, d][:], lhsT=kc[:].bitcast(FP8X4), lhsT_scale=ks[:],
+                    rhs=sc[:].bitcast(FP8X4), rhs_scale=sk[:], start=(h == 0), stop=(h == KH - 1),
+                )
+
+        def finish(i, d):
+            cols = slice(d * KP, (d + 1) * KP)
+            res[i, d] = ringed([P, KP], F32, "res", 6)
+            nc.vector.scalar_tensor_tensor(
+                out=res[i, d][:], in0=r_bank[i, d][:], scalar=nbeta[:, i : i + 1], in1=nbv[i, d][:],
+                op0=ALU.mult, op1=ALU.subtract,
+            )
+            nc.sync.dma_start(out=out_t[i][:, cols], in_=res[i, d][:])
+
+        widen_w(0, 0, on_vector=True)
+        pick_w_scales()
+        widen_w(0, 1)
+        turn_x(0)
+        group_w(0, 0)
+        widen_w(0, 2)
+        turn_x(1)
+        quant_w(0, 0)
+        group_w(0, 1)
+        widen_w(0, 3)
+        turn_x(2)
+        quant_w(0, 1)
+        group_w(0, 2)
+        empty_x(0)
+        quant_w(0, 2)
+        group_w(0, 3)
+        empty_x(1)
+        turn_x(3)
+        quant_x(0)
+        quant_w(0, 3)
+        empty_x(2)
+        quant_x(1)
+        spread_gain()
+        for i in range(TILES):
+            project(i, 0)
+            if i % 2 == 1 and i + 3 < TILES:
+                turn_x(i + 3)
+                turn_x(i + 4)
+            if i < XG:
+                widen_w(1, i)
+            if i + 3 < TILES:
+                empty_x(i + 3)
+            if i + 2 < TILES:
+                quant_x(i + 2)
+            if i == 3:
+                spread_state_scales()
+            if i >= 4:
+                widen_state(i - 4)
+            if i == 6:
+                for r in range(2):
+                    turn_state(r)
+                    empty_state(r)
+            if 1 <= i <= XG:
+                group_w(1, i - 1)
+            if i > 0:
+                quant_key(i - 1, 0)
+            make_key(i, 0)
+            if 1 <= i <= XG:
+                quant_w(1, i - 1)
+        reads = [(i, 0) for i in range(3)] + [(i - 3 * d, d) for i in range(3, TILES + 3) for d in range(DH) if i - 3 * d < TILES]
+        done = 0
+        for i in range(TILES + 1):
+            if i < TILES:
+                project(i, 1)
+            if i in (0, 2, 3):
+                for r in (2, 3) if i == 0 else (2 * i, 2 * i + 1):
+                    turn_state(r)
+                    empty_state(r)
+            if i == 0:
+                quant_key(TILES - 1, 0)
+            if i < 2:
+                widen_state(4 + 2 * i)
+                widen_state(5 + 2 * i, on_vector=True)
+            if 0 < i <= TILES:
+                quant_key(i - 1, 1)
+            if i < TILES:
+                make_key(i, 1)
+            if i in (1, 4):
+                quant_state(i // 4, 0)
+                quant_state(i // 4, 1)
+            n = 0 if i < 2 else 1 if i < 5 else 2
+            for (a, d) in reads[done : done + n]:
+                scale_v(a, d)
+                read_memory(a, d)
+                finish(a, d)
+            done = done + n
+        for (a, d) in reads[done:]:
+            scale_v(a, d)
+            read_memory(a, d)
+            finish(a, d)

@@ -24,6 +24,8 @@ XG = D // KP
 KH = DK // KP
 DH = DV // KP
 BANKS = 8
+XGB = 3
+PERM = False
 
 
 def tile_delta_memory_error_d7_kernel(tc, x, w_bytes, w_scale, gain, state_bytes, state_scale, v, beta, out):
@@ -86,23 +88,22 @@ def tile_delta_memory_error_d7_kernel(tc, x, w_bytes, w_scale, gain, state_bytes
         ss_col = kept([P, 1], F32, "sscol")
         nc.vector.memset(ss_col[:], 0.0)
         gain_col = kept([P, KH * PACK], BF16, "gaincol")
+        nc.scalar.dma_start(out=gain_col[:].rearrange("p (h t) -> p h t", t=PACK), in_=gain.rearrange("(h p t) -> p h t", p=P, t=PACK))
 
         load_w(0, 0)
         load_w(0, 1)
         load_x(0)
         load_w(0, 2)
         load_w(0, 3)
-        load_x(1)
-        nc.sync.dma_start(out=gain_col[:].rearrange("p (h t) -> p h t", t=PACK), in_=gain.rearrange("(h p t) -> p h t", p=P, t=PACK))
-        load_x(2)
+        for i in range(1, 4):
+            load_x(i)
+        nc.sync.dma_start(out=ss_col[0:64, :], in_=state_scale.rearrange("a (b o) -> (a b) o", o=1))
         for g in range(XG):
             load_w(1, g)
-            load_x(3 + g)
-            if g == 1:
-                nc.sync.dma_start(out=ss_col[0:64, :], in_=state_scale.rearrange("a (b o) -> (a b) o", o=1))
-        load_state(0)
-        load_x(7)
-        load_state(1)
+            if 4 + g < TILES:
+                load_x(4 + g)
+        for d in range(DH):
+            load_state(d)
         for i in range(TILES):
             load_v(i)
 
@@ -120,23 +121,26 @@ def tile_delta_memory_error_d7_kernel(tc, x, w_bytes, w_scale, gain, state_bytes
 
         w_wide, w_grp, w_codes, w_scales = {}, {}, {}, {}
 
-        def widen_w(h, g, on_vector=False):
+        def widen_w(h, g, vector_cols=0):
             w_wide[h, g] = ringed([P, PACK * KP], BF16, "wwide", 3)
-            if on_vector:
-                nc.vector.tensor_copy(out=w_wide[h, g][:], in_=w_raw[h, g][:].bitcast(FP8))
-            else:
-                nc.scalar.copy(out=w_wide[h, g][:], in_=w_raw[h, g][:].bitcast(FP8))
+            if vector_cols:
+                nc.vector.tensor_copy(out=w_wide[h, g][:, :vector_cols], in_=w_raw[h, g][:, :vector_cols].bitcast(FP8))
+            nc.scalar.copy(out=w_wide[h, g][:, vector_cols:], in_=w_raw[h, g][:, vector_cols:].bitcast(FP8))
 
-        def group_w(h, g):
-            w_grp[h, g] = ringed([P, PACK * KP], BF16, "wgrp", 2)
+        def group_w(h, g, on_scalar=0):
+            w_grp[h, g] = ringed([P, PACK * KP], BF16, "wgrp", 3)
             src = w_wide[h, g][:].rearrange("p (j m t) -> p m j t", j=PACK, t=PACK)
             dst = w_grp[h, g][:].rearrange("p (t m j) -> p m j t", j=PACK, t=PACK)
             for b in range(KP // SB):
                 col = g * 8 + h * 4 + b
-                nc.vector.tensor_scalar(
-                    out=dst[:, 32 * b : 32 * b + 32], in0=src[:, 32 * b : 32 * b + 32],
-                    scalar1=ws[:, col : col + 1], scalar2=None, op0=ALU.mult,
-                )
+                rows = slice(32 * b, 32 * b + 32)
+                if b < on_scalar:
+                    nc.scalar.activation(
+                        out=dst[:, rows].rearrange("p m j t -> p m t j"), in_=src[:, rows].rearrange("p m j t -> p m t j"),
+                        func=COPY, scale=ws[:, col : col + 1],
+                    )
+                else:
+                    nc.vector.tensor_scalar(out=dst[:, rows], in0=src[:, rows], scalar1=ws[:, col : col + 1], scalar2=None, op0=ALU.mult)
 
         def quantize(src, name):
             width = src.shape[1] // PACK
@@ -148,21 +152,23 @@ def tile_delta_memory_error_d7_kernel(tc, x, w_bytes, w_scale, gain, state_bytes
         def quant_w(h, g):
             w_codes[h, g], w_scales[h, g] = quantize(w_grp[h, g][:], "wq%d%d" % (h, g))
 
-        def turn(words):
+        def turn(words, sorted_words=False, warm_ups=0):
             bank = next_bank()
+            warm(bank, warm_ups)
             for n in range(4):
                 g, u = divmod(n, 2)
-                nc.tensor.transpose(bank[:, n * P : (n + 1) * P], words[:, 256 * g + u : 256 * (g + 1) : 2], ident[:])
+                src = words[:, n * P : (n + 1) * P] if sorted_words else words[:, 256 * g + u : 256 * (g + 1) : 2]
+                nc.tensor.transpose(bank[:, n * P : (n + 1) * P], src, ident[:])
             return bank
 
         x_bank, x_grp, x_q = {}, {}, {}
 
-        def turn_x(i):
+        def turn_x(i, warm_ups=0):
             for a in range(2):
-                x_bank[i, a] = turn(x_raw[i][:, a * KP : (a + 1) * KP])
+                x_bank[i, a] = turn(x_raw[i][:, a * KP : (a + 1) * KP], False, warm_ups)
 
         def empty_x(i):
-            x_grp[i] = ringed([P, D // 2], F32, "xgrp", 3)
+            x_grp[i] = ringed([P, D // 2], F32, "xgrp", XGB)
             for a in range(2):
                 nc.scalar.copy(
                     out=x_grp[i][:, a * KP : (a + 1) * KP].rearrange("p (g r u) -> p g r u", g=2, u=2),
@@ -174,14 +180,17 @@ def tile_delta_memory_error_d7_kernel(tc, x, w_bytes, w_scale, gain, state_bytes
 
         gain_wide = kept([P, KH * KP], BF16, "gainwide")
 
-        def spread_gain():
-            for h in range(KH):
-                nc.vector.tensor_copy(
-                    out=gain_wide[:, h * KP : (h + 1) * KP].rearrange("p (n t) -> p n t", t=PACK),
-                    in_=gain_col[:, h * PACK : (h + 1) * PACK].unsqueeze(1).to_broadcast([P, P, PACK]),
-                )
+        def spread_gain(h):
+            nc.scalar.copy(
+                out=gain_wide[:, h * KP : (h + 1) * KP].rearrange("p (n t) -> p n t", t=PACK),
+                in_=gain_col[:, h * PACK : (h + 1) * PACK].unsqueeze(1).to_broadcast([P, P, PACK]),
+            )
 
         h_bank, key, key_q = {}, {}, {}
+
+        def warm(bank, n):
+            for a in range(n):
+                nc.tensor.matmul(bank[:], lhsT=gain_wide[:, 0:P], rhs=gain_wide[:, 0:KP], start=True, stop=True)
 
         def project(i, h):
             h_bank[i, h] = next_bank()
@@ -198,40 +207,47 @@ def tile_delta_memory_error_d7_kernel(tc, x, w_bytes, w_scale, gain, state_bytes
                     )
 
         def make_key(i, h):
-            key[i, h] = ringed([P, KP], BF16, "key", 4)
+            if h == 0:
+                key[i] = kept([P, DK], BF16, "key%d" % i)
             nc.vector.scalar_tensor_tensor(
-                out=key[i, h][:].rearrange("p (n t) -> p n t", t=PACK),
+                out=key[i][:, h * KP : (h + 1) * KP].rearrange("p (n t) -> p n t", t=PACK),
                 in0=h_bank[i, h][:].rearrange("p (t n) -> p n t", t=PACK),
                 scalar=0.0,
                 in1=gain_wide[:, h * KP : (h + 1) * KP].rearrange("p (n t) -> p n t", t=PACK),
                 op0=ALU.max, op1=ALU.mult,
             )
 
-        def quant_key(i, h):
-            key_q[i, h] = quantize(key[i, h][:], "kq%d%d" % (i, h))
+        def quant_key(i):
+            key_q[i] = quantize(key[i][:], "kq%d" % i)
 
         ss = kept([P, 64], F32, "ss")
-        s_wide, s_bank, s_grp, s_q = {}, {}, {}, {}
+        s_wide, s_sorted, s_bank, s_grp, s_q = {}, {}, {}, {}, {}
 
         def spread_state_scales():
-            bank = next_bank()
-            nc.tensor.transpose(bank[:, 0:P], ss_col[:, 0:1].to_broadcast([P, P]), ident[:])
-            nc.scalar.copy(out=ss[:], in_=bank[:, 0:64])
+            s_bank["scales"] = next_bank()
+            nc.tensor.transpose(s_bank["scales"][:, 0:P], ss_col[:, 0:1].to_broadcast([P, P]), ident[:])
+
+        def take_state_scales():
+            nc.scalar.copy(out=ss[:], in_=s_bank["scales"][:, 0:64])
 
         def widen_state(r, on_vector=False):
             d, rr = divmod(r, PACK)
-            s_wide[r] = ringed([P, DK], BF16, "swide", 4)
+            s_wide[r] = ringed([P, DK], BF16, "swide", 5)
+            s_sorted[r] = on_vector and PERM
             for b in range(DK // SB):
                 src = s_raw[d][:, rr * DK + b * SB : rr * DK + (b + 1) * SB].bitcast(FP8)
                 dst = s_wide[r][:, b * SB : (b + 1) * SB]
                 col = r * 8 + b
                 if on_vector:
+                    if PERM:
+                        dst = s_wide[r][:].rearrange("p (h u q m e) -> p h q m u e", h=KH, u=2, q=4, e=2)[:, b // 4, b % 4]
+                        src = src.rearrange("p (m u e) -> p m u e", u=2, e=2)
                     nc.vector.tensor_scalar(out=dst, in0=src, scalar1=ss[:, col : col + 1], scalar2=None, op0=ALU.mult)
                 else:
                     nc.scalar.activation(out=dst, in_=src, func=COPY, scale=ss[:, col : col + 1])
 
         def turn_state(r):
-            s_bank[r] = turn(s_wide[r][:].bitcast(F32))
+            s_bank[r] = turn(s_wide[r][:].bitcast(F32), s_sorted[r])
 
         def empty_state(r):
             d, rr = divmod(r, PACK)
@@ -254,99 +270,93 @@ def tile_delta_memory_error_d7_kernel(tc, x, w_bytes, w_scale, gain, state_bytes
         def read_memory(i, d):
             r_bank[i, d] = next_bank()
             for h in range(KH):
-                kc, ks = key_q[i, h]
+                kc, ks = key_q[i]
+                toks = slice(h * P, (h + 1) * P)
                 sc, sk = s_q[d, h]
                 nc.tensor.matmul_mx(
-                    out=r_bank[i, d][:], lhsT=kc[:].bitcast(FP8X4), lhsT_scale=ks[:],
+                    out=r_bank[i, d][:], lhsT=kc[:, toks].bitcast(FP8X4), lhsT_scale=ks[:, toks],
                     rhs=sc[:].bitcast(FP8X4), rhs_scale=sk[:], start=(h == 0), stop=(h == KH - 1),
                 )
 
         def finish(i, d):
             cols = slice(d * KP, (d + 1) * KP)
-            res[i, d] = ringed([P, KP], F32, "res", 6)
+            if d == 0:
+                res[i] = keep.tile([P, DV], F32, name="res", tag="xwords%d" % i, align_bytes=64)
             nc.vector.scalar_tensor_tensor(
-                out=res[i, d][:], in0=r_bank[i, d][:], scalar=nbeta[:, i : i + 1], in1=nbv[i, d][:],
+                out=res[i][:, cols], in0=r_bank[i, d][:], scalar=nbeta[:, i : i + 1], in1=nbv[i, d][:],
                 op0=ALU.mult, op1=ALU.subtract,
             )
-            nc.sync.dma_start(out=out_t[i][:, cols], in_=res[i, d][:])
+            nc.sync.dma_start(out=out_t[i][:, cols], in_=res[i][:, cols])
 
-        widen_w(0, 0, on_vector=True)
+        HX = 4
         pick_w_scales()
-        widen_w(0, 1)
-        turn_x(0)
-        group_w(0, 0)
-        widen_w(0, 2)
-        turn_x(1)
-        quant_w(0, 0)
-        group_w(0, 1)
-        widen_w(0, 3)
-        turn_x(2)
-        quant_w(0, 1)
-        group_w(0, 2)
-        empty_x(0)
-        quant_w(0, 2)
-        group_w(0, 3)
-        empty_x(1)
-        turn_x(3)
+        spread_gain(0)
+        widen_w(0, 0, vector_cols=1024)
+        for g in range(XG):
+            turn_x(g, 0)
+            if g > 0:
+                widen_w(0, g)
+            group_w(0, g)
+            if g > 0:
+                quant_w(0, g - 1)
+        for i in range(3):
+            empty_x(i)
+        for i in range(XG, HX):
+            turn_x(i, 0)
         quant_x(0)
-        quant_w(0, 3)
-        empty_x(2)
+        quant_w(0, XG - 1)
         quant_x(1)
-        spread_gain()
+        quant_x(2)
         for i in range(TILES):
             project(i, 0)
-            if i % 2 == 1 and i + 3 < TILES:
-                turn_x(i + 3)
-                turn_x(i + 4)
+            if i + HX < TILES:
+                turn_x(i + HX)
+            if i == 0:
+                spread_state_scales()
             if i < XG:
                 widen_w(1, i)
             if i + 3 < TILES:
                 empty_x(i + 3)
-            if i + 2 < TILES:
-                quant_x(i + 2)
-            if i == 3:
-                spread_state_scales()
-            if i >= 4:
-                widen_state(i - 4)
+            if i == 1:
+                take_state_scales()
+            if i >= 3:
+                widen_state(i - 3)
             if i == 6:
-                for r in range(2):
+                for r in (0, 1):
                     turn_state(r)
                     empty_state(r)
-            if 1 <= i <= XG:
-                group_w(1, i - 1)
-            if i > 0:
-                quant_key(i - 1, 0)
+            if i < XG:
+                group_w(1, i)
+            if i + 3 < TILES:
+                quant_x(i + 3)
             make_key(i, 0)
-            if 1 <= i <= XG:
-                quant_w(1, i - 1)
-        reads = [(i, 0) for i in range(3)] + [(i - 3 * d, d) for i in range(3, TILES + 3) for d in range(DH) if i - 3 * d < TILES]
-        done = 0
+            if i < XG:
+                quant_w(1, i)
+        spread_gain(1)
+        todo = [(a, d) for d in range(DH) for a in range(TILES)]
+        TS, QS = (0, 1, 3), (1, 4)
         for i in range(TILES + 1):
+            if i < 3:
+                widen_state(5 + i, on_vector=True)
+            if i in TS:
+                first = 2 + 2 * TS.index(i)
+                for r in (first, first + 1):
+                    turn_state(r)
+                    empty_state(r)
             if i < TILES:
                 project(i, 1)
-            if i in (0, 2, 3):
-                for r in (2, 3) if i == 0 else (2 * i, 2 * i + 1):
-                    turn_state(r)
-                    empty_state(r)
-            if i == 0:
-                quant_key(TILES - 1, 0)
-            if i < 2:
-                widen_state(4 + 2 * i)
-                widen_state(5 + 2 * i, on_vector=True)
-            if 0 < i <= TILES:
-                quant_key(i - 1, 1)
+            if i > 0:
+                quant_key(i - 1)
+            if i in QS:
+                quant_state(QS.index(i), 0)
+                quant_state(QS.index(i), 1)
             if i < TILES:
                 make_key(i, 1)
-            if i in (1, 4):
-                quant_state(i // 4, 0)
-                quant_state(i // 4, 1)
-            n = 0 if i < 2 else 1 if i < 5 else 2
-            for (a, d) in reads[done : done + n]:
+            ready = sorted([(a, d) for (a, d) in todo if a < i and i > QS[d]])
+            if i < TILES:
+                ready = ready[:2]
+            for (a, d) in ready:
                 scale_v(a, d)
                 read_memory(a, d)
                 finish(a, d)
-            done = done + n
-        for (a, d) in reads[done:]:
-            scale_v(a, d)
-            read_memory(a, d)
-            finish(a, d)
+                todo.remove((a, d))

@@ -165,7 +165,7 @@ def tile_delta_memory_error_d7_kernel(tc, x, w_bytes, w_scale, gain, state_bytes
 
         def turn_x(i, warm_ups=0):
             for a in range(2):
-                x_bank[i, a] = turn(x_raw[i][:, a * KP : (a + 1) * KP], False, warm_ups)
+                x_bank[i, a] = turn(x_raw[i][:, a * KP : (a + 1) * KP], False, warm_ups[a] if warm_ups else 0)
 
         def empty_x(i):
             x_grp[i] = ringed([P, D // 2], F32, "xgrp", XGB)
@@ -190,7 +190,7 @@ def tile_delta_memory_error_d7_kernel(tc, x, w_bytes, w_scale, gain, state_bytes
 
         def warm(bank, n):
             for a in range(n):
-                nc.tensor.matmul(bank[:], lhsT=gain_wide[:, 0:P], rhs=gain_wide[:, 0:KP], start=True, stop=True)
+                nc.tensor.matmul(bank[:, 0:P], lhsT=ident[:], rhs=ident[:], start=True, stop=True)
 
         def project(i, h):
             h_bank[i, h] = next_bank()
@@ -293,7 +293,7 @@ def tile_delta_memory_error_d7_kernel(tc, x, w_bytes, w_scale, gain, state_bytes
         spread_gain(0)
         widen_w(0, 0, vector_cols=1024)
         for g in range(XG):
-            turn_x(g, 0)
+            turn_x(g, (7, 2) if g == 0 else (2, 1) if g == 1 else (1, 1))
             if g > 0:
                 widen_w(0, g)
             group_w(0, g)

@@ -16,16 +16,21 @@ ALU = mybir.AluOpType
 COPY = mybir.ActivationFunctionType.Copy
 
 P = 128
-PACK = 4
-KP = P * PACK
+SLOTS = 4
+KP = P * SLOTS
 SB = 128
+QUAD = SB // SLOTS
 TILES = T // P
-XG = D // KP
-KH = DK // KP
-DH = DV // KP
+PAIRS = TILES // 2
+PASSES = D // KP
+HALVES = DK // KP
+OUT_HALVES = DV // KP
+ROWS = DV // P
 BANKS = 8
-XGB = 3
-PERM = False
+
+FIRST_W_VECTOR_COLS = SLOTS * KP // 2
+STATE_ROWS_ON_SCALAR = 4
+X_AHEAD = BANKS // 2
 
 
 def tile_delta_memory_error_d7_kernel(tc, x, w_bytes, w_scale, gain, state_bytes, state_scale, v, beta, out):
@@ -35,328 +40,336 @@ def tile_delta_memory_error_d7_kernel(tc, x, w_bytes, w_scale, gain, state_bytes
     out_t = out.rearrange("(p i) c -> i p c", i=TILES)
 
     with ExitStack() as ctx:
-        keep = ctx.enter_context(tc.tile_pool(name="keep", bufs=1))
-        ring = ctx.enter_context(tc.tile_pool(name="ring", bufs=3))
+        sbuf = ctx.enter_context(tc.tile_pool(name="sbuf", bufs=1))
         psum = ctx.enter_context(tc.psum_pool(name="psum", bufs=1))
         ctx.enter_context(tc.manual_schedule())
 
         banks_taken = []
 
         def next_bank():
-            n = len(banks_taken)
-            bank = psum.tile([P, KP], F32, name="bank", tag="bank%d" % (n % BANKS))
-            banks_taken.append(n)
+            bank = psum.tile([P, KP], F32, name="bank", tag="bank%d" % (len(banks_taken) % BANKS))
+            banks_taken.append(bank)
             return bank
 
-        def kept(shape, dtype, name):
-            return keep.tile(shape, dtype, name=name, tag=name, align_bytes=64)
+        def new_tile(cols, dtype, name, tag=None, bufs=1):
+            return sbuf.tile([P, cols], dtype, name=name, tag=tag or name, bufs=bufs, align_bytes=64)
 
-        def ringed(shape, dtype, name, bufs):
-            return ring.tile(shape, dtype, name=name, tag=name, bufs=bufs, align_bytes=64)
-
-        w_raw, x_raw, s_raw, v_raw = {}, {}, {}, {}
+        w_raw, x_words, state_raw, v_sb = {}, {}, {}, {}
 
         def load_w(h, g):
-            w_raw[h, g] = kept([P, PACK * KP], U8, "wbytes%d%d" % (h, g))
+            w_raw[h, g] = new_tile(SLOTS * KP, U8, "w_bytes%d%d" % (h, g))
             nc.sync.dma_start(
-                out=w_raw[h, g][:].rearrange("p (j c) -> p j c", j=PACK),
-                in_=w_bytes[g * KP : (g + 1) * KP, h * KP : (h + 1) * KP].rearrange("(p j) c -> p j c", j=PACK),
+                out=w_raw[h, g][:].rearrange("p (j c) -> p j c", j=SLOTS),
+                in_=w_bytes[g * KP : (g + 1) * KP, h * KP : (h + 1) * KP].rearrange("(p j) c -> p j c", j=SLOTS),
             )
 
         def load_x(i):
-            x_raw[i] = kept([P, D // 2], F32, "xwords%d" % i)
-            nc.sync.dma_start(out=x_raw[i][:], in_=x_t[i].bitcast(F32))
+            x_words[i] = new_tile(D // 2, F32, "x_words%d" % i)
+            nc.sync.dma_start(out=x_words[i][:], in_=x_t[i].bitcast(F32))
 
         def load_state(d):
-            s_raw[d] = kept([P, PACK * DK], U8, "sbytes%d" % d)
+            state_raw[d] = new_tile(SLOTS * DK, U8, "state_bytes%d" % d)
             nc.sync.dma_start(
-                out=s_raw[d][:].rearrange("p (r k) -> p r k", r=PACK),
+                out=state_raw[d][:].rearrange("p (r k) -> p r k", k=DK),
                 in_=state_bytes[d * KP : (d + 1) * KP, :].rearrange("(r p) k -> p r k", p=P),
             )
 
         def load_v(i):
-            v_raw[i] = kept([P, DV], BF16, "v%d" % i)
-            nc.sync.dma_start(out=v_raw[i][:], in_=v_t[i])
+            v_sb[i] = new_tile(DV, BF16, "v%d" % i)
+            nc.sync.dma_start(out=v_sb[i][:], in_=v_t[i])
 
-        ident = kept([P, P], F32, "ident")
+        ident = new_tile(P, F32, "ident")
         make_identity(nc, ident[:])
 
-        beta_sb = kept([P, TILES], BF16, "beta")
+        beta_sb = new_tile(TILES, BF16, "beta")
         nc.scalar.dma_start(out=beta_sb[:], in_=beta.rearrange("(p i) o -> p (i o)", i=TILES))
-        ws_col = kept([P, 1], F32, "wscol")
-        nc.scalar.dma_start(out=ws_col[:], in_=w_scale.rearrange("a (b o) -> (a b) o", o=1))
-        ss_col = kept([P, 1], F32, "sscol")
-        nc.vector.memset(ss_col[:], 0.0)
-        gain_col = kept([P, KH * PACK], BF16, "gaincol")
-        nc.scalar.dma_start(out=gain_col[:].rearrange("p (h t) -> p h t", t=PACK), in_=gain.rearrange("(h p t) -> p h t", p=P, t=PACK))
+        w_scale_col = new_tile(1, F32, "w_scale_col")
+        nc.scalar.dma_start(out=w_scale_col[:], in_=w_scale.rearrange("a (b o) -> (a b) o", o=1))
+        state_scale_count = ROWS * (DK // SB)
+        state_scale_col = new_tile(1, F32, "state_scale_col")
+        nc.vector.memset(state_scale_col[:], 0.0)
+        gain_col = new_tile(HALVES * SLOTS, BF16, "gain_col")
+        nc.scalar.dma_start(
+            out=gain_col[:].rearrange("p (h t) -> p h t", t=SLOTS),
+            in_=gain.rearrange("(h p t) -> p h t", p=P, t=SLOTS),
+        )
 
         load_w(0, 0)
         load_w(0, 1)
         load_x(0)
         load_w(0, 2)
         load_w(0, 3)
-        for i in range(1, 4):
+        for i in range(1, X_AHEAD):
             load_x(i)
-        nc.sync.dma_start(out=ss_col[0:64, :], in_=state_scale.rearrange("a (b o) -> (a b) o", o=1))
-        for g in range(XG):
+        nc.sync.dma_start(out=state_scale_col[0:state_scale_count, :], in_=state_scale.rearrange("a (b o) -> (a b) o", o=1))
+        for g in range(PASSES):
             load_w(1, g)
-            if 4 + g < TILES:
-                load_x(4 + g)
-        for d in range(DH):
+            load_x(X_AHEAD + g)
+        for d in range(OUT_HALVES):
             load_state(d)
         for i in range(TILES):
             load_v(i)
 
-        nbeta = kept([P, TILES], F32, "nbeta")
-        nc.scalar.activation(out=nbeta[:], in_=beta_sb[:], func=COPY, scale=-1.0)
+        neg_beta = new_tile(TILES, F32, "neg_beta")
+        nc.scalar.activation(out=neg_beta[:], in_=beta_sb[:], func=COPY, scale=-1.0)
 
-        ws = kept([P, XG * 8], F32, "ws")
-        bank = next_bank()
-        nc.tensor.transpose(bank[:, 0:P], ws_col[:, 0:1].to_broadcast([P, P]), ident[:])
-        ws_spread = bank[:, 0:P].rearrange("p (g q b) -> p q g b", g=XG, q=4)
+        def spread_over_partitions(col):
+            bank = next_bank()
+            nc.tensor.transpose(bank[:, 0:P], col[:, 0:1].to_broadcast([P, P]), ident[:])
+            return bank
 
-        def pick_w_scales():
-            for q in range(4):
-                nc.vector.tensor_copy(out=ws[32 * q : 32 * q + 32, :].rearrange("p (g b) -> p g b", g=XG), in_=ws_spread[32 * q : 32 * q + 32, q])
+        def quantize(src, name):
+            cols = src.shape[1] // SLOTS
+            codes = new_tile(cols, U32, name + "_codes")
+            scales = new_tile(cols, U8, name + "_scales")
+            nc.vector.quantize_mx(out=codes[:].bitcast(FP8X4), scales=scales[:], in_=src)
+            return codes, scales
 
-        w_wide, w_grp, w_codes, w_scales = {}, {}, {}, {}
+        def matmul_pass(acc, stationary, m_cols, moving, n_cols, first, last):
+            nc.tensor.matmul_mx(
+                out=acc,
+                lhsT=stationary[0][:, m_cols].bitcast(FP8X4),
+                lhsT_scale=stationary[1][:, m_cols],
+                rhs=moving[0][:, n_cols].bitcast(FP8X4),
+                rhs_scale=moving[1][:, n_cols],
+                start=first,
+                stop=last,
+            )
+
+        def turn(words, sorted_words):
+            bank = next_bank()
+            for n in range(4):
+                g, u = divmod(n, 2)
+                src = words[:, n * P : (n + 1) * P] if sorted_words else words[:, 2 * P * g + u : 2 * P * (g + 1) : 2]
+                nc.tensor.transpose(bank[:, n * P : (n + 1) * P], src, ident[:])
+            return bank
+
+        col_blocks = DK // SB
+        w_scale_sb = new_tile(PASSES * col_blocks, F32, "w_scale_sb")
+        w_wide, w_grouped, w_q = {}, {}, {}
+
+        def spread_w_scales():
+            rows = spread_over_partitions(w_scale_col)[:, 0:P].rearrange("p (g q b) -> p q g b", g=PASSES, b=col_blocks)
+            for q in range(P // QUAD):
+                part = slice(QUAD * q, QUAD * (q + 1))
+                nc.vector.tensor_copy(out=w_scale_sb[part, :].rearrange("p (g b) -> p g b", g=PASSES), in_=rows[part, q])
 
         def widen_w(h, g, vector_cols=0):
-            w_wide[h, g] = ringed([P, PACK * KP], BF16, "wwide", 3)
+            w_wide[h, g] = new_tile(SLOTS * KP, BF16, "w_wide", bufs=4)
             if vector_cols:
                 nc.vector.tensor_copy(out=w_wide[h, g][:, :vector_cols], in_=w_raw[h, g][:, :vector_cols].bitcast(FP8))
             nc.scalar.copy(out=w_wide[h, g][:, vector_cols:], in_=w_raw[h, g][:, vector_cols:].bitcast(FP8))
 
-        def group_w(h, g, on_scalar=0):
-            w_grp[h, g] = ringed([P, PACK * KP], BF16, "wgrp", 3)
-            src = w_wide[h, g][:].rearrange("p (j m t) -> p m j t", j=PACK, t=PACK)
-            dst = w_grp[h, g][:].rearrange("p (t m j) -> p m j t", j=PACK, t=PACK)
+        def group_w(h, g):
+            w_grouped[h, g] = new_tile(SLOTS * KP, BF16, "w_grouped", bufs=3)
+            src = w_wide[h, g][:].rearrange("p (j m t) -> p m j t", j=SLOTS, t=SLOTS)
+            dst = w_grouped[h, g][:].rearrange("p (t m j) -> p m j t", j=SLOTS, t=SLOTS)
             for b in range(KP // SB):
-                col = g * 8 + h * 4 + b
-                rows = slice(32 * b, 32 * b + 32)
-                if b < on_scalar:
-                    nc.scalar.activation(
-                        out=dst[:, rows].rearrange("p m j t -> p m t j"), in_=src[:, rows].rearrange("p m j t -> p m t j"),
-                        func=COPY, scale=ws[:, col : col + 1],
-                    )
-                else:
-                    nc.vector.tensor_scalar(out=dst[:, rows], in0=src[:, rows], scalar1=ws[:, col : col + 1], scalar2=None, op0=ALU.mult)
-
-        def quantize(src, name):
-            width = src.shape[1] // PACK
-            codes = kept([P, width], U32, name + "c")
-            scales = kept([P, width], U8, name + "s")
-            nc.vector.quantize_mx(out=codes[:].bitcast(FP8X4), scales=scales[:], in_=src)
-            return codes, scales
+                col = g * col_blocks + h * (KP // SB) + b
+                ms = slice(QUAD * b, QUAD * (b + 1))
+                nc.vector.tensor_scalar(
+                    out=dst[:, ms], in0=src[:, ms], scalar1=w_scale_sb[:, col : col + 1], scalar2=None, op0=ALU.mult
+                )
 
         def quant_w(h, g):
-            w_codes[h, g], w_scales[h, g] = quantize(w_grp[h, g][:], "wq%d%d" % (h, g))
+            w_q[h, g] = quantize(w_grouped[h, g][:], "w%d%d" % (h, g))
 
-        def turn(words, sorted_words=False, warm_ups=0):
-            bank = next_bank()
-            warm(bank, warm_ups)
-            for n in range(4):
-                g, u = divmod(n, 2)
-                src = words[:, n * P : (n + 1) * P] if sorted_words else words[:, 256 * g + u : 256 * (g + 1) : 2]
-                nc.tensor.transpose(bank[:, n * P : (n + 1) * P], src, ident[:])
-            return bank
+        x_bank, x_grouped, x_q = {}, {}, {}
 
-        x_bank, x_grp, x_q = {}, {}, {}
-
-        def turn_x(i, warm_ups=0):
-            for a in range(2):
-                x_bank[i, a] = turn(x_raw[i][:, a * KP : (a + 1) * KP], False, warm_ups[a] if warm_ups else 0)
+        def turn_x(i):
+            for a in range(PASSES // 2):
+                x_bank[i, a] = turn(x_words[i][:, a * KP : (a + 1) * KP], False)
 
         def empty_x(i):
-            x_grp[i] = ringed([P, D // 2], F32, "xgrp", XGB)
-            for a in range(2):
+            pair, s = divmod(i, 2)
+            for a in range(PASSES // 2):
+                if s == 0:
+                    x_grouped[pair, a] = new_tile(2 * KP, F32, "x_grouped", bufs=4)
                 nc.scalar.copy(
-                    out=x_grp[i][:, a * KP : (a + 1) * KP].rearrange("p (g r u) -> p g r u", g=2, u=2),
+                    out=x_grouped[pair, a][:].rearrange("p (g s r u) -> p s g r u", g=2, s=2, u=2)[:, s],
                     in_=x_bank[i, a][:].rearrange("p (g u r) -> p g r u", g=2, u=2),
                 )
 
-        def quant_x(i):
-            x_q[i] = quantize(x_grp[i][:].bitcast(BF16), "xq%d" % i)
+        def quant_x(pair, a):
+            x_q[pair, a] = quantize(x_grouped[pair, a][:].bitcast(BF16), "x%d%d" % (pair, a))
 
-        gain_wide = kept([P, KH * KP], BF16, "gainwide")
+        gain_wide = new_tile(HALVES * KP, BF16, "gain_wide")
+        h_bank, key_planes, key, key_q = {}, {}, {}, {}
 
         def spread_gain(h):
             nc.scalar.copy(
-                out=gain_wide[:, h * KP : (h + 1) * KP].rearrange("p (n t) -> p n t", t=PACK),
-                in_=gain_col[:, h * PACK : (h + 1) * PACK].unsqueeze(1).to_broadcast([P, P, PACK]),
+                out=gain_wide[:, h * KP : (h + 1) * KP].rearrange("p (u n e) -> p u n e", u=2, e=2),
+                in_=gain_col[:, h * SLOTS : (h + 1) * SLOTS].rearrange("p (u e) -> p u e", u=2).unsqueeze(2).to_broadcast([P, 2, P, 2]),
             )
 
-        h_bank, key, key_q = {}, {}, {}
+        def project(pair, h, u):
+            h_bank[pair, h, u] = next_bank()
+            for e in range(2):
+                slot_cols = slice((2 * u + e) * P, (2 * u + e + 1) * P)
+                for g in range(PASSES):
+                    tokens = slice((g % 2) * 2 * P, (g % 2 + 1) * 2 * P)
+                    acc = h_bank[pair, h, u][:, e * 2 * P : (e + 1) * 2 * P]
+                    matmul_pass(acc, w_q[h, g], slot_cols, x_q[pair, g // 2], tokens, g == 0, g == PASSES - 1)
 
-        def warm(bank, n):
-            for a in range(n):
-                nc.tensor.matmul(bank[:, 0:P], lhsT=ident[:], rhs=ident[:], start=True, stop=True)
+        def make_key(pair, h, u):
+            if u == 0:
+                key_planes[pair, h] = new_tile(2 * KP, BF16, "key_planes", bufs=3)
+            gains = gain_wide[:, (2 * h + u) * 2 * P : (2 * h + u + 1) * 2 * P].rearrange("p (n e) -> p n e", e=2)
+            nc.vector.scalar_tensor_tensor(
+                out=key_planes[pair, h][:, u * KP : (u + 1) * KP].rearrange("p (s n e) -> p s n e", s=2, e=2),
+                in0=h_bank[pair, h, u][:].rearrange("p (e s n) -> p s n e", e=2, s=2),
+                scalar=0.0,
+                in1=gains.unsqueeze(1).to_broadcast([P, 2, P, 2]),
+                op0=ALU.max,
+                op1=ALU.mult,
+            )
 
-        def project(i, h):
-            h_bank[i, h] = next_bank()
-            xc, xs = x_q[i]
-            for t in range(PACK):
-                cols = slice(t * P, (t + 1) * P)
-                for g in range(XG):
-                    toks = slice(g * P, (g + 1) * P)
-                    nc.tensor.matmul_mx(
-                        out=h_bank[i, h][:, cols],
-                        lhsT=w_codes[h, g][:, cols].bitcast(FP8X4), lhsT_scale=w_scales[h, g][:, cols],
-                        rhs=xc[:, toks].bitcast(FP8X4), rhs_scale=xs[:, toks],
-                        start=(g == 0), stop=(g == XG - 1),
+        def weave_key(pair, h):
+            if h == 0:
+                key[pair] = new_tile(DK, F32, "key%d" % pair)
+            nc.scalar.copy(
+                out=key[pair][:].rearrange("p (s h n u) -> p h s n u", s=2, h=HALVES, u=2)[:, h],
+                in_=key_planes[pair, h][:].bitcast(F32).rearrange("p (u s n) -> p s n u", u=2, s=2),
+            )
+
+        def quant_key(pair):
+            key_q[pair] = quantize(key[pair][:].bitcast(BF16), "key%d" % pair)
+
+        state_scale_sb = new_tile(state_scale_count, F32, "state_scale_sb")
+        state_wide, state_grouped, state_q = {}, {}, {}
+
+        def widen_state(r):
+            d, rr = divmod(r, SLOTS)
+            state_wide[r] = new_tile(DK, BF16, "state_wide", bufs=6)
+            for b in range(col_blocks):
+                src = state_raw[d][:, rr * DK + b * SB : rr * DK + (b + 1) * SB].bitcast(FP8)
+                scale = state_scale_sb[:, r * col_blocks + b : r * col_blocks + b + 1]
+                if r < STATE_ROWS_ON_SCALAR:
+                    nc.scalar.activation(out=state_wide[r][:, b * SB : (b + 1) * SB], in_=src, func=COPY, scale=scale)
+                else:
+                    h, q = divmod(b, KP // SB)
+                    dst = state_wide[r][:].rearrange("p (h u q m e) -> p h q m u e", h=HALVES, u=2, m=QUAD, e=2)[:, h, q]
+                    nc.vector.tensor_scalar(
+                        out=dst, in0=src.rearrange("p (m u e) -> p m u e", u=2, e=2), scalar1=scale, scalar2=None, op0=ALU.mult
                     )
 
-        def make_key(i, h):
-            if h == 0:
-                key[i] = kept([P, DK], BF16, "key%d" % i)
-            nc.vector.scalar_tensor_tensor(
-                out=key[i][:, h * KP : (h + 1) * KP].rearrange("p (n t) -> p n t", t=PACK),
-                in0=h_bank[i, h][:].rearrange("p (t n) -> p n t", t=PACK),
-                scalar=0.0,
-                in1=gain_wide[:, h * KP : (h + 1) * KP].rearrange("p (n t) -> p n t", t=PACK),
-                op0=ALU.max, op1=ALU.mult,
-            )
-
-        def quant_key(i):
-            key_q[i] = quantize(key[i][:], "kq%d" % i)
-
-        ss = kept([P, 64], F32, "ss")
-        s_wide, s_sorted, s_bank, s_grp, s_q = {}, {}, {}, {}, {}
-
-        def spread_state_scales():
-            s_bank["scales"] = next_bank()
-            nc.tensor.transpose(s_bank["scales"][:, 0:P], ss_col[:, 0:1].to_broadcast([P, P]), ident[:])
-
-        def take_state_scales():
-            nc.scalar.copy(out=ss[:], in_=s_bank["scales"][:, 0:64])
-
-        def widen_state(r, on_vector=False):
-            d, rr = divmod(r, PACK)
-            s_wide[r] = ringed([P, DK], BF16, "swide", 5)
-            s_sorted[r] = on_vector and PERM
-            for b in range(DK // SB):
-                src = s_raw[d][:, rr * DK + b * SB : rr * DK + (b + 1) * SB].bitcast(FP8)
-                dst = s_wide[r][:, b * SB : (b + 1) * SB]
-                col = r * 8 + b
-                if on_vector:
-                    if PERM:
-                        dst = s_wide[r][:].rearrange("p (h u q m e) -> p h q m u e", h=KH, u=2, q=4, e=2)[:, b // 4, b % 4]
-                        src = src.rearrange("p (m u e) -> p m u e", u=2, e=2)
-                    nc.vector.tensor_scalar(out=dst, in0=src, scalar1=ss[:, col : col + 1], scalar2=None, op0=ALU.mult)
-                else:
-                    nc.scalar.activation(out=dst, in_=src, func=COPY, scale=ss[:, col : col + 1])
-
         def turn_state(r):
-            s_bank[r] = turn(s_wide[r][:].bitcast(F32), s_sorted[r])
-
-        def empty_state(r):
-            d, rr = divmod(r, PACK)
+            d, rr = divmod(r, SLOTS)
+            bank = turn(state_wide[r][:].bitcast(F32), r >= STATE_ROWS_ON_SCALAR)
             if rr == 0:
-                s_grp[d] = kept([P, KH * KP * 2], F32, "sgrp%d" % d)
+                state_grouped[d] = new_tile(HALVES * 2 * KP, F32, "state_grouped%d" % d)
             nc.scalar.copy(
-                out=s_grp[d][:].rearrange("p (h a r u) -> p a h r u", h=KH, a=PACK, u=2)[:, rr],
-                in_=s_bank[r][:].rearrange("p (h u r) -> p h r u", h=KH, u=2),
+                out=state_grouped[d][:].rearrange("p (h a r u) -> p a h r u", h=HALVES, r=P, u=2)[:, rr],
+                in_=bank[:].rearrange("p (h u r) -> p h r u", h=HALVES, u=2),
             )
 
-        def quant_state(d, h):
-            s_q[d, h] = quantize(s_grp[d][:, h * 2 * KP : (h + 1) * 2 * KP].bitcast(BF16), "sq%d%d" % (d, h))
+        def quant_state(d):
+            for h in range(HALVES):
+                src = state_grouped[d][:, h * 2 * KP : (h + 1) * 2 * KP].bitcast(BF16)
+                state_q[d, h] = quantize(src, "state%d%d" % (d, h))
 
-        nbv, r_bank, res = {}, {}, {}
+        result = {}
 
         def scale_v(i, d):
-            nbv[i, d] = ringed([P, KP], F32, "nbv", 6)
-            nc.scalar.activation(out=nbv[i, d][:], in_=v_raw[i][:, d * KP : (d + 1) * KP], func=COPY, scale=nbeta[:, i : i + 1])
-
-        def read_memory(i, d):
-            r_bank[i, d] = next_bank()
-            for h in range(KH):
-                kc, ks = key_q[i]
-                toks = slice(h * P, (h + 1) * P)
-                sc, sk = s_q[d, h]
-                nc.tensor.matmul_mx(
-                    out=r_bank[i, d][:], lhsT=kc[:, toks].bitcast(FP8X4), lhsT_scale=ks[:, toks],
-                    rhs=sc[:].bitcast(FP8X4), rhs_scale=sk[:], start=(h == 0), stop=(h == KH - 1),
-                )
-
-        def finish(i, d):
-            cols = slice(d * KP, (d + 1) * KP)
             if d == 0:
-                res[i] = keep.tile([P, DV], F32, name="res", tag="xwords%d" % i, align_bytes=64)
-            nc.vector.scalar_tensor_tensor(
-                out=res[i][:, cols], in0=r_bank[i, d][:], scalar=nbeta[:, i : i + 1], in1=nbv[i, d][:],
-                op0=ALU.mult, op1=ALU.subtract,
-            )
-            nc.sync.dma_start(out=out_t[i][:, cols], in_=res[i][:, cols])
+                result[i] = new_tile(DV, F32, "result", tag="x_words%d" % i)
+            cols = slice(d * KP, (d + 1) * KP)
+            nc.scalar.activation(out=result[i][:, cols], in_=v_sb[i][:, cols], func=COPY, scale=neg_beta[:, i : i + 1])
 
-        HX = 4
-        pick_w_scales()
+        def read_and_store(i, d):
+            bank = next_bank()
+            for h in range(HALVES):
+                tokens = slice((HALVES * (i % 2) + h) * P, (HALVES * (i % 2) + h + 1) * P)
+                matmul_pass(bank[:], key_q[i // 2], tokens, state_q[d, h], slice(0, KP), h == 0, h == HALVES - 1)
+            cols = slice(d * KP, (d + 1) * KP)
+            nc.vector.scalar_tensor_tensor(
+                out=result[i][:, cols],
+                in0=bank[:],
+                scalar=neg_beta[:, i : i + 1],
+                in1=result[i][:, cols],
+                op0=ALU.mult,
+                op1=ALU.subtract,
+            )
+            nc.sync.dma_start(out=out_t[i][:, cols], in_=result[i][:, cols])
+
+        spread_w_scales()
         spread_gain(0)
-        widen_w(0, 0, vector_cols=1024)
-        for g in range(XG):
-            turn_x(g, (7, 2) if g == 0 else (2, 1) if g == 1 else (1, 1))
+        widen_w(0, 0, FIRST_W_VECTOR_COLS)
+        for g in range(PASSES):
+            turn_x(g)
             if g > 0:
                 widen_w(0, g)
             group_w(0, g)
             if g > 0:
                 quant_w(0, g - 1)
-        for i in range(3):
+        for i in range(X_AHEAD - 1):
             empty_x(i)
-        for i in range(XG, HX):
-            turn_x(i, 0)
-        quant_x(0)
-        quant_w(0, XG - 1)
-        quant_x(1)
-        quant_x(2)
-        for i in range(TILES):
-            project(i, 0)
-            if i + HX < TILES:
-                turn_x(i + HX)
-            if i == 0:
-                spread_state_scales()
-            if i < XG:
-                widen_w(1, i)
-            if i + 3 < TILES:
-                empty_x(i + 3)
-            if i == 1:
-                take_state_scales()
-            if i >= 3:
-                widen_state(i - 3)
-            if i == 6:
-                for r in (0, 1):
-                    turn_state(r)
-                    empty_state(r)
-            if i < XG:
-                group_w(1, i)
-            if i + 3 < TILES:
-                quant_x(i + 3)
-            make_key(i, 0)
-            if i < XG:
-                quant_w(1, i)
-        spread_gain(1)
-        todo = [(a, d) for d in range(DH) for a in range(TILES)]
-        TS, QS = (0, 1, 3), (1, 4)
-        for i in range(TILES + 1):
-            if i < 3:
-                widen_state(5 + i, on_vector=True)
-            if i in TS:
-                first = 2 + 2 * TS.index(i)
-                for r in (first, first + 1):
-                    turn_state(r)
-                    empty_state(r)
-            if i < TILES:
-                project(i, 1)
-            if i > 0:
-                quant_key(i - 1)
-            if i in QS:
-                quant_state(QS.index(i), 0)
-                quant_state(QS.index(i), 1)
-            if i < TILES:
-                make_key(i, 1)
-            ready = sorted([(a, d) for (a, d) in todo if a < i and i > QS[d]])
-            if i < TILES:
-                ready = ready[:2]
-            for (a, d) in ready:
-                scale_v(a, d)
-                read_memory(a, d)
-                finish(a, d)
-                todo.remove((a, d))
+        quant_x(0, 0)
+        quant_w(0, PASSES - 1)
+        quant_x(0, 1)
+
+        for k in range(2 * (PAIRS - 1)):
+            pair, u = divmod(k, 2)
+            project(pair, 0, u)
+            if k + X_AHEAD < TILES:
+                turn_x(k + X_AHEAD)
+            if k == 0:
+                state_scale_bank = spread_over_partitions(state_scale_col)
+            if k < PASSES:
+                widen_w(1, k)
+            if k + X_AHEAD - 1 < TILES:
+                empty_x(k + X_AHEAD - 1)
+            if k == 1:
+                nc.scalar.copy(out=state_scale_sb[:], in_=state_scale_bank[:, 0:state_scale_count])
+                spread_gain(1)
+            if u == 0 and pair > 0:
+                weave_key(pair - 1, 0)
+            if k >= PASSES - 1:
+                widen_state(k - (PASSES - 1))
+            if k < PASSES:
+                group_w(1, k)
+            if u == 0:
+                quant_x(pair + 1, 0)
+                quant_x(pair + 1, 1)
+            make_key(pair, 0, u)
+            if k < PASSES:
+                quant_w(1, k)
+
+        halves_left = [(0, 1), (PAIRS - 1, 0)] + [(pair, 1) for pair in range(1, PAIRS)]
+        projections = [(pair, h, u) for pair, h in halves_left for u in range(2)]
+        state_widened = 2 * (PAIRS - 1) - (PASSES - 1)
+        outputs = [(pair, d) for pair in range(PAIRS) for d in range(OUT_HALVES)]
+        first_scale, second_read = 3, 6
+        unwoven = (PAIRS - 2, 0)
+        for n in range(second_read + len(outputs) - 1):
+            if n < len(projections):
+                project(*projections[n])
+            if 1 <= n <= ROWS // 2:
+                turn_state(2 * n - 2)
+                turn_state(2 * n - 1)
+            woven, unwoven = unwoven, None
+            if woven:
+                weave_key(*woven)
+            for r in range(state_widened + 2 * n, min(state_widened + 2 * n + 2, ROWS)):
+                widen_state(r)
+            if first_scale <= n < first_scale + len(outputs):
+                pair, d = outputs[n - first_scale]
+                scale_v(2 * pair, d)
+                scale_v(2 * pair + 1, d)
+            if n in (first_scale, second_read - 1):
+                quant_state(0 if n == first_scale else 1)
+            if n < len(projections):
+                make_key(*projections[n])
+                if projections[n][2] == 1:
+                    unwoven = projections[n][:2]
+            reading = None
+            if n == first_scale + 1:
+                reading = outputs[0]
+            elif n >= second_read:
+                reading = outputs[n - second_read + 1]
+            if reading:
+                read_and_store(2 * reading[0], reading[1])
+            if woven and woven[1] == HALVES - 1:
+                quant_key(woven[0])
+            if reading:
+                read_and_store(2 * reading[0] + 1, reading[1])

from contextlib import ExitStack

import concourse.mybir as mybir
from concourse.masks import make_identity

T, D, DK, DV = 1024, 2048, 1024, 1024
FLOPS = 2 * T * D * DK + 2 * T * DK * DV

F32 = mybir.dt.float32
BF16 = mybir.dt.bfloat16
U32 = mybir.dt.uint32
U8 = mybir.dt.uint8
FP8 = mybir.dt.float8_e4m3fn
FP8X4 = mybir.dt.float8_e4m3fn_x4
ALU = mybir.AluOpType
COPY = mybir.ActivationFunctionType.Copy

P = 128
SLOTS = 4
KP = P * SLOTS
SB = 128
QUAD = SB // SLOTS
TILES = T // P
PAIRS = TILES // 2
PASSES = D // KP
HALVES = DK // KP
OUT_HALVES = DV // KP
ROWS = DV // P
BANKS = 8

FIRST_W_VECTOR_COLS = SLOTS * KP // 2
STATE_ROWS_ON_SCALAR = 4
X_AHEAD = BANKS // 2


def tile_delta_memory_error_d7_kernel(tc, x, w_bytes, w_scale, gain, state_bytes, state_scale, v, beta, out):
    nc = tc.nc
    x_t = x.rearrange("(p i) k -> i p k", i=TILES)
    v_t = v.rearrange("(p i) c -> i p c", i=TILES)
    out_t = out.rearrange("(p i) c -> i p c", i=TILES)

    with ExitStack() as ctx:
        sbuf = ctx.enter_context(tc.tile_pool(name="sbuf", bufs=1))
        psum = ctx.enter_context(tc.psum_pool(name="psum", bufs=1))
        ctx.enter_context(tc.manual_schedule())

        banks_taken = []

        def next_bank():
            bank = psum.tile([P, KP], F32, name="bank", tag="bank%d" % (len(banks_taken) % BANKS))
            banks_taken.append(bank)
            return bank

        def new_tile(cols, dtype, name, tag=None, bufs=1):
            return sbuf.tile([P, cols], dtype, name=name, tag=tag or name, bufs=bufs, align_bytes=64)

        w_raw, x_words, state_raw, v_sb = {}, {}, {}, {}

        def load_w(h, g):
            w_raw[h, g] = new_tile(SLOTS * KP, U8, "w_bytes%d%d" % (h, g))
            nc.sync.dma_start(
                out=w_raw[h, g][:].rearrange("p (j c) -> p j c", j=SLOTS),
                in_=w_bytes[g * KP : (g + 1) * KP, h * KP : (h + 1) * KP].rearrange("(p j) c -> p j c", j=SLOTS),
            )

        def load_x(i):
            x_words[i] = new_tile(D // 2, F32, "x_words%d" % i)
            nc.sync.dma_start(out=x_words[i][:], in_=x_t[i].bitcast(F32))

        def load_state(d):
            state_raw[d] = new_tile(SLOTS * DK, U8, "state_bytes%d" % d)
            nc.sync.dma_start(
                out=state_raw[d][:].rearrange("p (r k) -> p r k", k=DK),
                in_=state_bytes[d * KP : (d + 1) * KP, :].rearrange("(r p) k -> p r k", p=P),
            )

        def load_v(i):
            v_sb[i] = new_tile(DV, BF16, "v%d" % i)
            nc.sync.dma_start(out=v_sb[i][:], in_=v_t[i])

        ident = new_tile(P, F32, "ident")
        make_identity(nc, ident[:])

        beta_sb = new_tile(TILES, BF16, "beta")
        nc.scalar.dma_start(out=beta_sb[:], in_=beta.rearrange("(p i) o -> p (i o)", i=TILES))
        w_scale_col = new_tile(1, F32, "w_scale_col")
        nc.scalar.dma_start(out=w_scale_col[:], in_=w_scale.rearrange("a (b o) -> (a b) o", o=1))
        state_scale_count = ROWS * (DK // SB)
        state_scale_col = new_tile(1, F32, "state_scale_col")
        nc.vector.memset(state_scale_col[:], 0.0)
        gain_col = new_tile(HALVES * SLOTS, BF16, "gain_col")
        nc.scalar.dma_start(
            out=gain_col[:].rearrange("p (h t) -> p h t", t=SLOTS),
            in_=gain.rearrange("(h p t) -> p h t", p=P, t=SLOTS),
        )

        load_w(0, 0)
        load_w(0, 1)
        load_x(0)
        load_w(0, 2)
        load_w(0, 3)
        for i in range(1, X_AHEAD):
            load_x(i)
        nc.sync.dma_start(out=state_scale_col[0:state_scale_count, :], in_=state_scale.rearrange("a (b o) -> (a b) o", o=1))
        for g in range(PASSES):
            load_w(1, g)
            load_x(X_AHEAD + g)
        for d in range(OUT_HALVES):
            load_state(d)
        for i in range(TILES):
            load_v(i)

        neg_beta = new_tile(TILES, F32, "neg_beta")
        nc.scalar.activation(out=neg_beta[:], in_=beta_sb[:], func=COPY, scale=-1.0)

        def spread_over_partitions(col):
            bank = next_bank()
            nc.tensor.transpose(bank[:, 0:P], col[:, 0:1].to_broadcast([P, P]), ident[:])
            return bank

        def quantize(src, name):
            cols = src.shape[1] // SLOTS
            codes = new_tile(cols, U32, name + "_codes")
            scales = new_tile(cols, U8, name + "_scales")
            nc.vector.quantize_mx(out=codes[:].bitcast(FP8X4), scales=scales[:], in_=src)
            return codes, scales

        def matmul_pass(acc, stationary, m_cols, moving, n_cols, first, last):
            nc.tensor.matmul_mx(
                out=acc,
                lhsT=stationary[0][:, m_cols].bitcast(FP8X4),
                lhsT_scale=stationary[1][:, m_cols],
                rhs=moving[0][:, n_cols].bitcast(FP8X4),
                rhs_scale=moving[1][:, n_cols],
                start=first,
                stop=last,
            )

        def turn(words, sorted_words):
            bank = next_bank()
            for n in range(4):
                g, u = divmod(n, 2)
                src = words[:, n * P : (n + 1) * P] if sorted_words else words[:, 2 * P * g + u : 2 * P * (g + 1) : 2]
                nc.tensor.transpose(bank[:, n * P : (n + 1) * P], src, ident[:])
            return bank

        col_blocks = DK // SB
        w_scale_sb = new_tile(PASSES * col_blocks, F32, "w_scale_sb")
        w_wide, w_grouped, w_q = {}, {}, {}

        def spread_w_scales():
            rows = spread_over_partitions(w_scale_col)[:, 0:P].rearrange("p (g q b) -> p q g b", g=PASSES, b=col_blocks)
            for q in range(P // QUAD):
                part = slice(QUAD * q, QUAD * (q + 1))
                nc.vector.tensor_copy(out=w_scale_sb[part, :].rearrange("p (g b) -> p g b", g=PASSES), in_=rows[part, q])

        def widen_w(h, g, vector_cols=0):
            w_wide[h, g] = new_tile(SLOTS * KP, BF16, "w_wide", bufs=4)
            if vector_cols:
                nc.vector.tensor_copy(out=w_wide[h, g][:, :vector_cols], in_=w_raw[h, g][:, :vector_cols].bitcast(FP8))
            nc.scalar.copy(out=w_wide[h, g][:, vector_cols:], in_=w_raw[h, g][:, vector_cols:].bitcast(FP8))

        def group_w(h, g):
            w_grouped[h, g] = new_tile(SLOTS * KP, BF16, "w_grouped", bufs=3)
            src = w_wide[h, g][:].rearrange("p (j m t) -> p m j t", j=SLOTS, t=SLOTS)
            dst = w_grouped[h, g][:].rearrange("p (t m j) -> p m j t", j=SLOTS, t=SLOTS)
            for b in range(KP // SB):
                col = g * col_blocks + h * (KP // SB) + b
                ms = slice(QUAD * b, QUAD * (b + 1))
                nc.vector.tensor_scalar(
                    out=dst[:, ms], in0=src[:, ms], scalar1=w_scale_sb[:, col : col + 1], scalar2=None, op0=ALU.mult
                )

        def quant_w(h, g):
            w_q[h, g] = quantize(w_grouped[h, g][:], "w%d%d" % (h, g))

        x_bank, x_grouped, x_q = {}, {}, {}

        def turn_x(i):
            for a in range(PASSES // 2):
                x_bank[i, a] = turn(x_words[i][:, a * KP : (a + 1) * KP], False)

        def empty_x(i):
            pair, s = divmod(i, 2)
            for a in range(PASSES // 2):
                if s == 0:
                    x_grouped[pair, a] = new_tile(2 * KP, F32, "x_grouped", bufs=4)
                nc.scalar.copy(
                    out=x_grouped[pair, a][:].rearrange("p (g s r u) -> p s g r u", g=2, s=2, u=2)[:, s],
                    in_=x_bank[i, a][:].rearrange("p (g u r) -> p g r u", g=2, u=2),
                )

        def quant_x(pair, a):
            x_q[pair, a] = quantize(x_grouped[pair, a][:].bitcast(BF16), "x%d%d" % (pair, a))

        gain_wide = new_tile(HALVES * KP, BF16, "gain_wide")
        h_bank, key_planes, key, key_q = {}, {}, {}, {}

        def spread_gain(h):
            nc.scalar.copy(
                out=gain_wide[:, h * KP : (h + 1) * KP].rearrange("p (u n e) -> p u n e", u=2, e=2),
                in_=gain_col[:, h * SLOTS : (h + 1) * SLOTS].rearrange("p (u e) -> p u e", u=2).unsqueeze(2).to_broadcast([P, 2, P, 2]),
            )

        def project(pair, h, u):
            h_bank[pair, h, u] = next_bank()
            for e in range(2):
                slot_cols = slice((2 * u + e) * P, (2 * u + e + 1) * P)
                for g in range(PASSES):
                    tokens = slice((g % 2) * 2 * P, (g % 2 + 1) * 2 * P)
                    acc = h_bank[pair, h, u][:, e * 2 * P : (e + 1) * 2 * P]
                    matmul_pass(acc, w_q[h, g], slot_cols, x_q[pair, g // 2], tokens, g == 0, g == PASSES - 1)

        def make_key(pair, h, u):
            if u == 0:
                key_planes[pair, h] = new_tile(2 * KP, BF16, "key_planes", bufs=3)
            gains = gain_wide[:, (2 * h + u) * 2 * P : (2 * h + u + 1) * 2 * P].rearrange("p (n e) -> p n e", e=2)
            nc.vector.scalar_tensor_tensor(
                out=key_planes[pair, h][:, u * KP : (u + 1) * KP].rearrange("p (s n e) -> p s n e", s=2, e=2),
                in0=h_bank[pair, h, u][:].rearrange("p (e s n) -> p s n e", e=2, s=2),
                scalar=0.0,
                in1=gains.unsqueeze(1).to_broadcast([P, 2, P, 2]),
                op0=ALU.max,
                op1=ALU.mult,
            )

        def weave_key(pair, h):
            if h == 0:
                key[pair] = new_tile(DK, F32, "key%d" % pair)
            nc.scalar.copy(
                out=key[pair][:].rearrange("p (s h n u) -> p h s n u", s=2, h=HALVES, u=2)[:, h],
                in_=key_planes[pair, h][:].bitcast(F32).rearrange("p (u s n) -> p s n u", u=2, s=2),
            )

        def quant_key(pair):
            key_q[pair] = quantize(key[pair][:].bitcast(BF16), "key%d" % pair)

        state_scale_sb = new_tile(state_scale_count, F32, "state_scale_sb")
        state_wide, state_grouped, state_q = {}, {}, {}

        def widen_state(r):
            d, rr = divmod(r, SLOTS)
            state_wide[r] = new_tile(DK, BF16, "state_wide", bufs=6)
            for b in range(col_blocks):
                src = state_raw[d][:, rr * DK + b * SB : rr * DK + (b + 1) * SB].bitcast(FP8)
                scale = state_scale_sb[:, r * col_blocks + b : r * col_blocks + b + 1]
                if r < STATE_ROWS_ON_SCALAR:
                    nc.scalar.activation(out=state_wide[r][:, b * SB : (b + 1) * SB], in_=src, func=COPY, scale=scale)
                else:
                    h, q = divmod(b, KP // SB)
                    dst = state_wide[r][:].rearrange("p (h u q m e) -> p h q m u e", h=HALVES, u=2, m=QUAD, e=2)[:, h, q]
                    nc.vector.tensor_scalar(
                        out=dst, in0=src.rearrange("p (m u e) -> p m u e", u=2, e=2), scalar1=scale, scalar2=None, op0=ALU.mult
                    )

        def turn_state(r):
            d, rr = divmod(r, SLOTS)
            bank = turn(state_wide[r][:].bitcast(F32), r >= STATE_ROWS_ON_SCALAR)
            if rr == 0:
                state_grouped[d] = new_tile(HALVES * 2 * KP, F32, "state_grouped%d" % d)
            nc.scalar.copy(
                out=state_grouped[d][:].rearrange("p (h a r u) -> p a h r u", h=HALVES, r=P, u=2)[:, rr],
                in_=bank[:].rearrange("p (h u r) -> p h r u", h=HALVES, u=2),
            )

        def quant_state(d):
            for h in range(HALVES):
                src = state_grouped[d][:, h * 2 * KP : (h + 1) * 2 * KP].bitcast(BF16)
                state_q[d, h] = quantize(src, "state%d%d" % (d, h))

        result = {}

        def scale_v(i, d):
            if d == 0:
                result[i] = new_tile(DV, F32, "result", tag="x_words%d" % i)
            cols = slice(d * KP, (d + 1) * KP)
            nc.scalar.activation(out=result[i][:, cols], in_=v_sb[i][:, cols], func=COPY, scale=neg_beta[:, i : i + 1])

        def read_and_store(i, d):
            bank = next_bank()
            for h in range(HALVES):
                tokens = slice((HALVES * (i % 2) + h) * P, (HALVES * (i % 2) + h + 1) * P)
                matmul_pass(bank[:], key_q[i // 2], tokens, state_q[d, h], slice(0, KP), h == 0, h == HALVES - 1)
            cols = slice(d * KP, (d + 1) * KP)
            nc.vector.scalar_tensor_tensor(
                out=result[i][:, cols],
                in0=bank[:],
                scalar=neg_beta[:, i : i + 1],
                in1=result[i][:, cols],
                op0=ALU.mult,
                op1=ALU.subtract,
            )
            nc.sync.dma_start(out=out_t[i][:, cols], in_=result[i][:, cols])

        spread_w_scales()
        spread_gain(0)
        widen_w(0, 0, FIRST_W_VECTOR_COLS)
        for g in range(PASSES):
            turn_x(g)
            if g > 0:
                widen_w(0, g)
            group_w(0, g)
            if g > 0:
                quant_w(0, g - 1)
        for i in range(X_AHEAD - 1):
            empty_x(i)
        quant_x(0, 0)
        quant_w(0, PASSES - 1)
        quant_x(0, 1)

        for k in range(2 * (PAIRS - 1)):
            pair, u = divmod(k, 2)
            project(pair, 0, u)
            if k + X_AHEAD < TILES:
                turn_x(k + X_AHEAD)
            if k == 0:
                state_scale_bank = spread_over_partitions(state_scale_col)
            if k < PASSES:
                widen_w(1, k)
            if k + X_AHEAD - 1 < TILES:
                empty_x(k + X_AHEAD - 1)
            if k == 1:
                nc.scalar.copy(out=state_scale_sb[:], in_=state_scale_bank[:, 0:state_scale_count])
                spread_gain(1)
            if u == 0 and pair > 0:
                weave_key(pair - 1, 0)
            if k >= PASSES - 1:
                widen_state(k - (PASSES - 1))
            if k < PASSES:
                group_w(1, k)
            if u == 0:
                quant_x(pair + 1, 0)
                quant_x(pair + 1, 1)
            make_key(pair, 0, u)
            if k < PASSES:
                quant_w(1, k)

        halves_left = [(0, 1), (PAIRS - 1, 0)] + [(pair, 1) for pair in range(1, PAIRS)]
        projections = [(pair, h, u) for pair, h in halves_left for u in range(2)]
        state_widened = 2 * (PAIRS - 1) - (PASSES - 1)
        outputs = [(pair, d) for pair in range(PAIRS) for d in range(OUT_HALVES)]
        first_scale, second_read = 3, 6
        unwoven = (PAIRS - 2, 0)
        for n in range(second_read + len(outputs) - 1):
            if n < len(projections):
                project(*projections[n])
            if 1 <= n <= ROWS // 2:
                turn_state(2 * n - 2)
                turn_state(2 * n - 1)
            woven, unwoven = unwoven, None
            if woven:
                weave_key(*woven)
            for r in range(state_widened + 2 * n, min(state_widened + 2 * n + 2, ROWS)):
                widen_state(r)
            if first_scale <= n < first_scale + len(outputs):
                pair, d = outputs[n - first_scale]
                scale_v(2 * pair, d)
                scale_v(2 * pair + 1, d)
            if n in (first_scale, second_read - 1):
                quant_state(0 if n == first_scale else 1)
            if n < len(projections):
                make_key(*projections[n])
                if projections[n][2] == 1:
                    unwoven = projections[n][:2]
            reading = None
            if n == first_scale + 1:
                reading = outputs[0]
            elif n >= second_read:
                reading = outputs[n - second_read + 1]
            if reading:
                read_and_store(2 * reading[0], reading[1])
            if woven and woven[1] == HALVES - 1:
                quant_key(woven[0])
            if reading:
                read_and_store(2 * reading[0] + 1, reading[1])
